import numpy as np, ml_dtypes
CORES = [2,3,42,43,82,83,122,123]
N = 8
import mx_ref
BF = ml_dtypes.bfloat16
def entries(a):
    return np.ascontiguousarray(a.T).reshape(-1)
def table(e):
    return np.ascontiguousarray(np.reshape(e, (-1, 16)).T).astype(np.int32)
def cols(t, e):
    v = np.concatenate([t.reshape(128, -1, 4), np.zeros((128, 1, 4), BF)], axis=1)
    return np.ascontiguousarray(v[:, e]).reshape(128, -1)
def cut(t, i, w=512):
    return t[:, w * i:w * i + w]
def f(rng, *shape):
    return mx_ref.flush((rng.standard_normal(shape, dtype=np.float32) * np.exp2(rng.integers(-2, 3, shape[:-1] + (1,)))).astype(BF))
def wide(rng, *shape, cols=0):
    v = rng.standard_normal(shape, dtype=np.float32) * np.exp2(rng.integers(-12, 13, shape)).astype(np.float32)
    if cols: v *= np.repeat(np.exp2(rng.integers(-cols, cols + 1, shape[:-2] + (1, shape[-1] // 4))) * (rng.random(shape[:-2] + (1, shape[-1] // 4)) > 0.0625), 4, axis=-1).astype(np.float32)
    return mx_ref.flush(v.astype(BF))
T, K, O, CAPP = 512, 8, 1, 64
def lists(rng, foreign=False, own=False, same=False, absent=False):
    S = np.full((N, N, CAPP), -1); M = []
    for s in range(N):
        for d in range(N):
            n = CAPP if foreign else rng.integers(1, CAPP + 1)
            if s != d: S[s, d, rng.permutation(CAPP)[:n]] = rng.integers(0, T, n)
    k = np.arange(K)[:, None]
    for r in range(N):
        far = T + np.flatnonzero(S[:, r].reshape(-1) >= 0)
        m = np.where(rng.random((K, T)) < (1.0 if foreign else np.divide(k + 1, K + 1)), rng.choice(far, (K, T)), rng.integers(0, T, (K, T)))
        there = np.zeros((K, T), bool); there[rng.integers(0, K, T), np.arange(T)] = True
        if absent: there.reshape(-1)[rng.permutation(np.flatnonzero(~there))[:K * T - 2 * K * T // 3 - T]] = True
        else: there |= rng.random((K, T)) >= 0.1 + 0.5 * np.divide(k, K - 1)
        m = np.repeat(m[:, :1], T, axis=1) if same else np.where(there, m, -1)
        if own: m = np.stack([rng.permutation(T) for _ in range(K)])
        M.append(table(m))
    return {"send": np.stack([table(S[s]) for s in range(N)]), "mp": np.stack(M)}
def setup_inputs(rng):
    return {"x": f(rng, N, 128, 4 * T), "w": f(rng, N, 128, K * O * 512), **lists(rng)}
def setup_inputs_absent(rng):
    return {**setup_inputs(rng), **lists(rng, absent=True)}
def setup_inputs_foreign(rng):
    return {**setup_inputs(rng), **lists(rng, foreign=True)}
def setup_inputs_same(rng):
    return {**setup_inputs(rng), **lists(rng, same=True)}
def setup_inputs_spread(rng):
    d = setup_inputs(rng); d["x"] = wide(rng, N, 128, 4 * T); return d
def setup_inputs_own(rng):
    return {**setup_inputs(rng), **lists(rng, own=True)}
def check_inputs(d):
    b = []
    for n in ("x", "w"):
        a = np.abs(d[n].astype(np.float32))
        if not np.isfinite(a).all() or ((a > 0) & ((a < 2.0 ** -30) | (a > 2.0 ** 30))).any(): b.append(n)
    for r in range(N):
        s, m = entries(d["send"][r]), entries(d["mp"][r]).reshape(K, T)
        if s.min() < -1 or s.max() >= T or (s[r * CAPP:(r + 1) * CAPP] != -1).any(): b.append("send")
        held = np.concatenate([entries(d["send"][q])[r * CAPP:(r + 1) * CAPP] for q in range(N)])
        if m.min() < -1 or m.max() >= T + N * CAPP or (held[m[m >= T] - T] < 0).any() or (m < 0).all(axis=0).any(): b.append("mp")
    return b
def reference(x, w, send, mp):
    y = np.zeros((N, 128, O * T), np.float32)
    for r in range(N):
        held = [cols(x[s], entries(send[s])[r * CAPP:(r + 1) * CAPP]) for s in range(N)]
        v = np.concatenate([x[r]] + held, axis=1)
        m = entries(mp[r]).reshape(K, T)
        for k in range(K):
            q = mx_ref.quantize(cols(v, m[k]))
            for o in range(O): y[r][:, T * o:T * o + T] += mx_ref.matmul(mx_ref.quantize(cut(w[r], k * O + o)), q)
    return {"y": y}

@@ -1,0 +1,254 @@
+from concourse.bass import DstId, RemoteDMATransfer
+from concourse.mybir import dt, AluOpType, ActivationFunctionType
+
+COLS, MAPS, CAP = 512, 8, 64
+STRIDE = 1028
+WIN = 1 + 2 * COLS
+FAR, NEAR = 5 * CAP, 2 * CAP
+
+SCRATCH = {
+    "xt": ("sbuf", [128, 4 * COLS], "bfloat16"),
+    "wt": ("sbuf", [128, 512 * MAPS], "bfloat16"),
+    "ls": ("sbuf", [128, 32], "int32"),
+    "lm": ("sbuf", [128, 256], "int32"),
+    "offs": ("sbuf", [128, 32], "uint16"),
+    "offm": ("sbuf", [128, 256], "uint16"),
+    "h": ("sbuf", [128, 4 * 7 * CAP], "bfloat16"),
+    "hq": ("sbuf", [128, 7 * CAP], "float8_e4m3fn_x4"),
+    "hp": ("sbuf", [128, 7 * CAP], "uint8"),
+    "xq": ("sbuf", [128, COLS], "float8_e4m3fn_x4"),
+    "xp": ("sbuf", [128, COLS], "uint8"),
+    "wq": ("sbuf", [128, 128 * MAPS], "float8_e4m3fn_x4"),
+    "wp": ("sbuf", [128, 128 * MAPS], "uint8"),
+    "aq": ("sbuf", [128, FAR], "float8_e4m3fn_x4"),
+    "ap": ("sbuf", [128, FAR], "uint8"),
+    "bq": ("sbuf", [128, NEAR], "float8_e4m3fn_x4"),
+    "bp": ("sbuf", [128, NEAR], "uint8"),
+    "win": ("sbuf", [128, STRIDE * MAPS], "float32"),
+    "g0": ("sbuf", [128, COLS], "float32"),
+    "g2": ("sbuf", [128, COLS], "float32"),
+    "acc0": ("sbuf", [128, COLS], "float32"),
+    "acc1": ("sbuf", [128, COLS], "float32"),
+    "yt": ("sbuf", [128, COLS], "float32"),
+    "ps": ("psum", [128, 512 * MAPS], "float32"),
+}
+SEMAPHORES = ["sl", "sx", "sw0", "sw1", "sm", "sy", "cv", "cs", "ct", "arra", "arrb", "loc"]
+
+
+def groups(T, topo, r):
+    me = topo.chip(T.cores[r])
+    far, near, mate = [], [], []
+    for s in range(len(T.cores)):
+        c = topo.chip(T.cores[s])
+        if s == r:
+            continue
+        if c == me:
+            mate.append(s)
+        elif topo.same_plane(me, c):
+            near.append(s)
+        else:
+            far.append(s)
+    return far, near, mate
+
+
+def runs(ranks):
+    out = []
+    for i, s in enumerate(ranks):
+        if out and out[-1][1] + out[-1][2] == s:
+            out[-1] = (out[-1][0], out[-1][1], out[-1][2] + 1)
+        else:
+            out.append((i, s, 1))
+    return out
+
+
+def mask_of(engines):
+    m = 0
+    for e in engines:
+        m |= 1 << e
+    return m
+
+
+def rank_program(g, core, T, topo):
+    r = T.rank_of(core)
+    if r is None:
+        return
+    sem = T.sem
+    V, S, P, Y = g.vector, g.scalar, g.tensor, g.sync
+    Copy = ActivationFunctionType.Copy
+    cnt = {"cv": 0, "cs": 0, "ct": 0}
+    seen = {}
+
+    def wait(name, q, s, n):
+        if seen.get((name, s), 0) < n:
+            q.wait_ge(sem[s], n)
+            seen[(name, s)] = n
+
+    def inc(s, call):
+        call.then_inc(sem[s], 1)
+        cnt[s] += 1
+        return cnt[s]
+
+    def wv(s, n):
+        wait("V", V, s, n)
+
+    def ws(s, n):
+        wait("S", S, s, n)
+
+    far, near, mate = groups(T, topo, r)
+    dests = far + near + mate
+    nfar = len(far) * CAP
+
+    for i in range(4):
+        Y.dma_start(T.ls[16 * i:16 * i + 16, :], T.send[:, :]).then_inc(sem.sl, 16)
+        S.dma_start(T.ls[64 + 16 * i:80 + 16 * i, :], T.send[:, :]).then_inc(sem.sl, 16)
+    Y.dma_start(T.xt[:, 0:1024], T.x[:, 0:1024]).then_inc(sem.sx, 16)
+    S.dma_start(T.xt[:, 1024:2048], T.x[:, 1024:2048]).then_inc(sem.sx, 16)
+    Y.dma_start(T.wt[:, 0:2048], T.w[:, 0:2048]).then_inc(sem.sw0, 16)
+    Y.dma_start(T.wt[:, 2048:4096], T.w[:, 2048:4096]).then_inc(sem.sw1, 16)
+    for i in range(8):
+        Y.dma_start(T.lm[16 * i:16 * i + 16, :], T.mp[:, :]).then_inc(sem.sm, 16)
+
+    for k in range(MAPS):
+        inc("cv", V.memset(T.win[:, k * STRIDE:k * STRIDE + 1], 0.0))
+        o = k * STRIDE + 1 + COLS + CAP * r
+        zeros = inc("cv", V.memset(T.win[:, o:o + CAP], 0.0))
+
+    wv("sl", 128)
+    for i, d, n in runs(far) + [(len(far) + a, b, c) for a, b, c in runs(near)] + \
+            [(len(far) + len(near) + a, b, c) for a, b, c in runs(mate)]:
+        offs = inc("cv", V.tensor_scalar(T.offs[:, 4 * i:4 * (i + n)], T.ls[:, 4 * d:4 * (d + n)], 4.0, 0.0,
+                                         AluOpType.mult, AluOpType.max))
+
+    blocks = []
+    for lo, hi in ((0, nfar), (nfar, 7 * CAP)):
+        for q, (name, eng) in enumerate((("V", V), ("S", S))):
+            wait(name, eng, "cv", offs)
+            wait(name, eng, "sx", 32)
+            for t in (2 * q, 2 * q + 1):
+                out = T.h[:, 4 * lo + t:4 * hi:4]
+                src = T.xt[:, t:4 * COLS].indirect(T.offs[:, lo // 16:hi // 16])
+                if q == 0:
+                    gv = inc("cv", V.tensor_copy(out, src))
+                else:
+                    gs = inc("cs", S.activation(out, src, Copy))
+        wv("cv", gv)
+        wv("cs", gs)
+        blocks.append(inc("cv", V.quantize_mx(T.hq[:, lo:hi], T.hp[:, lo:hi], T.h[:, 4 * lo:4 * hi])))
+
+    def transfer(d, engines, codes):
+        dfar, dnear, dmate = groups(T, topo, d)
+        rid, pid, _ = topo.addr(T.cores[d])
+        a = CAP * dests.index(d)
+        if r in dnear:
+            p, land, plane, arr = CAP * dnear.index(r), T.bq, T.bp, sem.arrb
+        else:
+            p, land, plane, arr = CAP * sorted(dfar + dmate).index(r), T.aq, T.ap, sem.arra
+        if codes:
+            src, dst = T.hq[:, a:a + CAP].bitcast(dt.uint8), land[:, p:p + CAP].bitcast(dt.uint8)
+        else:
+            src, dst = T.hp[:, a:a + CAP], plane[:, p:p + CAP]
+        return RemoteDMATransfer(dst_ids=[DstId(rid=rid, pnc=pid)], dma_engine_mask=mask_of(engines),
+                                 remote_sem=arr, src=src, dst=dst)
+
+    out_engines = topo.engines(core, T.cores[far[0]])
+    home_engines = [e for e in topo.engines(core, T.cores[mate[0]]) if e not in out_engines]
+    local = 0
+    for ranks, home, ready in ((far, [], blocks[0]), (near, mate, blocks[1])):
+        wait("G", g, "cv", ready)
+        w = len(out_engines) // len(ranks)
+        for codes in (True, False):
+            tr = [transfer(d, out_engines[w * i:w * i + w], codes) for i, d in enumerate(ranks)]
+            tr += [transfer(d, home_engines, codes) for d in home]
+            g.remote_dma_fused(tr, local_sem=sem.loc)
+            local += w * len(ranks) + len(home_engines) * len(home)
+
+    xq = inc("cv", V.quantize_mx(T.xq[:, :], T.xp[:, :], T.xt[:, :]))
+    wq = []
+    for i in range(2):
+        wv("sw%d" % i, 16)
+        wq.append(inc("cv", V.quantize_mx(T.wq[:, 512 * i:512 * i + 512], T.wp[:, 512 * i:512 * i + 512],
+                                          T.wt[:, 2048 * i:2048 * i + 2048])))
+    wv("sm", 128)
+    offm = inc("cv", V.tensor_scalar(T.offm[:, :], T.lm[:, :], 1.0, None, AluOpType.add))
+
+    def product(k, q, p, n):
+        return inc("ct", P.matmul_mx(T.ps[:, 512 * k:512 * k + n], T.wq[:, 128 * k:128 * k + 128],
+                                     T.wp[:, 128 * k:128 * k + 128], q[:, 0:n], p[:, 0:n], True, True))
+
+    def copy(k, a, to, n, vector):
+        dst, src = T.win[:, k * STRIDE + to:k * STRIDE + to + n], T.ps[:, 512 * k + a:512 * k + a + n]
+        if vector:
+            return "cv", inc("cv", V.tensor_copy(dst, src))
+        return "cs", inc("cs", S.activation(dst, src, Copy))
+
+    done = [None] * MAPS
+    for k in range(MAPS):
+        wait("P", P, "cv", wq[k // 4])
+        m = product(k, T.xq, T.xp, COLS)
+        (wv if k % 2 == 0 else ws)("ct", m)
+        done[k] = copy(k, 0, 1, COLS, k % 2 == 0)
+    wait("P", P, "arra", 2 * len(out_engines) // len(far) * len(far) + 2 * len(home_engines))
+    first = sorted(far + mate)
+    for k in range(MAPS):
+        wait("P", P, *done[k])
+        m = product(k, T.aq, T.ap, FAR)
+        (wv if k % 2 == 0 else ws)("ct", m)
+        for i, s, n in runs(first):
+            done[k] = copy(k, CAP * i, 1 + COLS + CAP * s, CAP * n, k % 2 == 0)
+    wait("P", P, "arrb", 2 * len(out_engines) // len(near) * len(near))
+    last = []
+    for k in range(MAPS):
+        wait("P", P, *done[k])
+        last.append(product(k, T.bq, T.bp, NEAR))
+    slots = 1 + COLS + CAP * near[0]
+    full = {}
+
+    def finish(k, vector):
+        (wv if vector else ws)("ct", last[k])
+        full[k] = [done[k], copy(k, 0, slots, NEAR, vector)]
+
+    def ready(name, eng, k):
+        wait(name, eng, "cv", offm)
+        wait(name, eng, "cv", zeros)
+        for s, n in full[k]:
+            wait(name, eng, s, n)
+
+    def pick(k, a=0, b=COLS):
+        return T.win[:, k * STRIDE:k * STRIDE + WIN].indirect(T.offm[:, 32 * k + a // 16:32 * k + b // 16])
+
+    finish(0, False)
+    finish(1, True)
+    half = COLS // 2
+    ready("S", S, 0)
+    a0 = inc("cs", S.activation(T.g0[:, 0:half], pick(0, 0, half), Copy))
+    ready("V", V, 0)
+    a1 = inc("cv", V.tensor_copy(T.g0[:, half:], pick(0, half, COLS)))
+    finish(3, False)
+    finish(2, False)
+    ready("S", S, 2)
+    a2 = inc("cs", S.activation(T.g2[:, :], pick(2), Copy))
+    for k in (4, 5, 6, 7):
+        finish(k, False)
+
+    def add(k, out, other):
+        ready("V", V, k)
+        return inc("cv", V.tensor_tensor(out[:, :], pick(k), other[:, :], AluOpType.add))
+
+    wv("cs", a0)
+    wv("cv", a1)
+    c0 = add(1, T.acc0, T.g0)
+    wv("cs", a2)
+    c1 = add(3, T.acc1, T.g2)
+    for k0, k1 in ((4, 5), (6, 7)):
+        wv("cv", c0)
+        c0 = add(k0, T.acc0, T.acc0)
+        wv("cv", c1)
+        c1 = add(k1, T.acc1, T.acc1)
+    wv("cv", c1)
+    for i, (name, eng) in enumerate((("Y", Y), ("S", S))):
+        c = slice(half * i, half * i + half)
+        n = inc("cv", V.tensor_tensor(T.yt[:, c], T.acc0[:, c], T.acc1[:, c], AluOpType.add))
+        wait(name, eng, "cv", n)
+        eng.dma_start(T.y[:, c], T.yt[:, c]).then_inc(sem.sy, 16)
+    wait("G", g, "loc", local)
+    Y.wait_ge(sem.sy, 32)

@@ -4,7 +4,8 @@ from concourse.mybir import dt, AluOpType, ActivationFunctionType
 COLS, MAPS, CAP = 512, 8, 64
 STRIDE = 1028
 WIN = 1 + 2 * COLS
-FAR, NEAR = 5 * CAP, 2 * CAP
+HALF = COLS // 2
+EARLY = ((0, "S"), (1, "V"), (2, "V"))
 
 SCRATCH = {
     "xt": ("sbuf", [128, 4 * COLS], "bfloat16"),
@@ -20,35 +21,29 @@ SCRATCH = {
     "xp": ("sbuf", [128, COLS], "uint8"),
     "wq": ("sbuf", [128, 128 * MAPS], "float8_e4m3fn_x4"),
     "wp": ("sbuf", [128, 128 * MAPS], "uint8"),
-    "aq": ("sbuf", [128, FAR], "float8_e4m3fn_x4"),
-    "ap": ("sbuf", [128, FAR], "uint8"),
-    "bq": ("sbuf", [128, NEAR], "float8_e4m3fn_x4"),
-    "bp": ("sbuf", [128, NEAR], "uint8"),
+    "aq": ("sbuf", [128, 7 * CAP], "float8_e4m3fn_x4"),
+    "ap": ("sbuf", [128, 7 * CAP], "uint8"),
     "win": ("sbuf", [128, STRIDE * MAPS], "float32"),
     "g0": ("sbuf", [128, COLS], "float32"),
-    "g2": ("sbuf", [128, COLS], "float32"),
-    "acc0": ("sbuf", [128, COLS], "float32"),
-    "acc1": ("sbuf", [128, COLS], "float32"),
-    "yt": ("sbuf", [128, COLS], "float32"),
+    "acc": ("sbuf", [128, COLS], "float32"),
     "ps": ("psum", [128, 512 * MAPS], "float32"),
 }
-SEMAPHORES = ["sl", "sx", "sw0", "sw1", "sm", "sy", "cv", "cs", "ct", "arra", "arrb", "loc"]
+SEMAPHORES = ["sl", "sx", "sw0", "sw1", "sw2", "sm", "sy", "cv", "cs", "ct", "arra", "arrb", "loc"]
 
 
 def groups(T, topo, r):
     me = topo.chip(T.cores[r])
     far, near, mate = [], [], []
-    for s in range(len(T.cores)):
+    for i in range(1, len(T.cores)):
+        s = (r + i) % len(T.cores)
         c = topo.chip(T.cores[s])
-        if s == r:
-            continue
         if c == me:
             mate.append(s)
         elif topo.same_plane(me, c):
             near.append(s)
         else:
             far.append(s)
-    return far, near, mate
+    return far, sorted(near), mate
 
 
 def runs(ranks):
@@ -74,37 +69,35 @@ def rank_program(g, core, T, topo):
         return
     sem = T.sem
     V, S, P, Y = g.vector, g.scalar, g.tensor, g.sync
+    queue = {"V": V, "S": S, "P": P, "Y": Y, "G": g}
     Copy = ActivationFunctionType.Copy
     cnt = {"cv": 0, "cs": 0, "ct": 0}
     seen = {}
 
-    def wait(name, q, s, n):
+    def wait(name, s, n):
         if seen.get((name, s), 0) < n:
-            q.wait_ge(sem[s], n)
+            queue[name].wait_ge(sem[s], n)
             seen[(name, s)] = n
 
     def inc(s, call):
         call.then_inc(sem[s], 1)
         cnt[s] += 1
-        return cnt[s]
-
-    def wv(s, n):
-        wait("V", V, s, n)
-
-    def ws(s, n):
-        wait("S", S, s, n)
+        return s, cnt[s]
 
     far, near, mate = groups(T, topo, r)
     dests = far + near + mate
-    nfar = len(far) * CAP
+    cut = len(far) // 2
+    first = sorted(far + mate)
+    order = first + near
 
     for i in range(4):
         Y.dma_start(T.ls[16 * i:16 * i + 16, :], T.send[:, :]).then_inc(sem.sl, 16)
         S.dma_start(T.ls[64 + 16 * i:80 + 16 * i, :], T.send[:, :]).then_inc(sem.sl, 16)
     Y.dma_start(T.xt[:, 0:1024], T.x[:, 0:1024]).then_inc(sem.sx, 16)
     S.dma_start(T.xt[:, 1024:2048], T.x[:, 1024:2048]).then_inc(sem.sx, 16)
-    Y.dma_start(T.wt[:, 0:2048], T.w[:, 0:2048]).then_inc(sem.sw0, 16)
-    Y.dma_start(T.wt[:, 2048:4096], T.w[:, 2048:4096]).then_inc(sem.sw1, 16)
+    wparts = ((0, 2), (2, 4), (4, 8))
+    for i, (a, b) in enumerate(wparts):
+        Y.dma_start(T.wt[:, 512 * a:512 * b], T.w[:, 512 * a:512 * b]).then_inc(sem["sw%d" % i], 16)
     for i in range(8):
         Y.dma_start(T.lm[16 * i:16 * i + 16, :], T.mp[:, :]).then_inc(sem.sm, 16)
 
@@ -113,142 +106,129 @@ def rank_program(g, core, T, topo):
         o = k * STRIDE + 1 + COLS + CAP * r
         zeros = inc("cv", V.memset(T.win[:, o:o + CAP], 0.0))
 
-    wv("sl", 128)
-    for i, d, n in runs(far) + [(len(far) + a, b, c) for a, b, c in runs(near)] + \
-            [(len(far) + len(near) + a, b, c) for a, b, c in runs(mate)]:
+    wait("V", "sl", 128)
+    for i, d, n in runs(dests):
         offs = inc("cv", V.tensor_scalar(T.offs[:, 4 * i:4 * (i + n)], T.ls[:, 4 * d:4 * (d + n)], 4.0, 0.0,
                                          AluOpType.mult, AluOpType.max))
 
-    blocks = []
-    for lo, hi in ((0, nfar), (nfar, 7 * CAP)):
-        for q, (name, eng) in enumerate((("V", V), ("S", S))):
-            wait(name, eng, "cv", offs)
-            wait(name, eng, "sx", 32)
-            for t in (2 * q, 2 * q + 1):
-                out = T.h[:, 4 * lo + t:4 * hi:4]
-                src = T.xt[:, t:4 * COLS].indirect(T.offs[:, lo // 16:hi // 16])
-                if q == 0:
-                    gv = inc("cv", V.tensor_copy(out, src))
-                else:
-                    gs = inc("cs", S.activation(out, src, Copy))
-        wv("cv", gv)
-        wv("cs", gs)
-        blocks.append(inc("cv", V.quantize_mx(T.hq[:, lo:hi], T.hp[:, lo:hi], T.h[:, 4 * lo:4 * hi])))
+    def gather(name, lo, hi, t):
+        wait(name, *offs)
+        wait(name, "sx", 32)
+        out = T.h[:, 4 * lo + t:4 * hi:4]
+        src = T.xt[:, t:4 * COLS].indirect(T.offs[:, lo // 16:hi // 16])
+        if name == "V":
+            return inc("cv", V.tensor_copy(out, src))
+        return inc("cs", S.activation(out, src, Copy))
+
+    def pack(lo, hi, parts):
+        for p in parts:
+            wait("V", *p)
+        return inc("cv", V.quantize_mx(T.hq[:, lo:hi], T.hp[:, lo:hi], T.h[:, 4 * lo:4 * hi]))
+
+    def pack_w(i):
+        a, b = wparts[i]
+        wait("V", "sw%d" % i, 16)
+        n = inc("cv", V.quantize_mx(T.wq[:, 128 * a:128 * b], T.wp[:, 128 * a:128 * b], T.wt[:, 512 * a:512 * b]))
+        return {k: n for k in range(a, b)}
+
+    b1, b2, b3 = CAP * cut, CAP * len(far), CAP * len(dests)
+    parts = [gather("V", 0, b1, 0), gather("V", 0, b1, 1), gather("S", 0, b1, 2), gather("S", 0, b1, 3)]
+    packed1 = pack(0, b1, parts)
+    parts = [gather("V", b1, b2, 0), gather("V", b1, b2, 1), gather("S", b1, b2, 2), gather("S", b1, b2, 3)]
+    packed2 = pack(b1, b2, parts)
+    parts = [gather("V", b2, b3, 0)] + [gather("S", b2, b3, t) for t in (1, 2, 3)]
+    xq = inc("cv", V.quantize_mx(T.xq[:, :], T.xp[:, :], T.xt[:, :]))
+    packed3 = pack(b2, b3, parts)
+    wq = pack_w(0)
+    wq.update(pack_w(1))
+    wq.update(pack_w(2))
+    wait("V", "sm", 128)
+    offm = inc("cv", V.tensor_scalar(T.offm[:, :], T.lm[:, :], 1.0, None, AluOpType.add))
+
+    out_engines = topo.engines(core, T.cores[far[0]])
+    home_engines = [e for e in topo.engines(core, T.cores[mate[0]]) if e not in out_engines][:2]
 
     def transfer(d, engines, codes):
         dfar, dnear, dmate = groups(T, topo, d)
         rid, pid, _ = topo.addr(T.cores[d])
         a = CAP * dests.index(d)
-        if r in dnear:
-            p, land, plane, arr = CAP * dnear.index(r), T.bq, T.bp, sem.arrb
-        else:
-            p, land, plane, arr = CAP * sorted(dfar + dmate).index(r), T.aq, T.ap, sem.arra
+        p = CAP * (sorted(dfar + dmate) + dnear).index(r)
         if codes:
-            src, dst = T.hq[:, a:a + CAP].bitcast(dt.uint8), land[:, p:p + CAP].bitcast(dt.uint8)
+            src, dst = T.hq[:, a:a + CAP].bitcast(dt.uint8), T.aq[:, p:p + CAP].bitcast(dt.uint8)
         else:
-            src, dst = T.hp[:, a:a + CAP], plane[:, p:p + CAP]
+            src, dst = T.hp[:, a:a + CAP], T.ap[:, p:p + CAP]
         return RemoteDMATransfer(dst_ids=[DstId(rid=rid, pnc=pid)], dma_engine_mask=mask_of(engines),
-                                 remote_sem=arr, src=src, dst=dst)
+                                 remote_sem=sem.arrb if r in dnear else sem.arra, src=src, dst=dst)
 
-    out_engines = topo.engines(core, T.cores[far[0]])
-    home_engines = [e for e in topo.engines(core, T.cores[mate[0]]) if e not in out_engines]
-    local = 0
-    for ranks, home, ready in ((far, [], blocks[0]), (near, mate, blocks[1])):
-        wait("G", g, "cv", ready)
-        w = len(out_engines) // len(ranks)
-        for codes in (True, False):
-            tr = [transfer(d, out_engines[w * i:w * i + w], codes) for i, d in enumerate(ranks)]
-            tr += [transfer(d, home_engines, codes) for d in home]
-            g.remote_dma_fused(tr, local_sem=sem.loc)
-            local += w * len(ranks) + len(home_engines) * len(home)
+    local, comes_a, comes_b = 0, 0, 0
+    for ranks, home, codes, packed in ((far[:cut], [], True, packed1), (far[cut:], [], True, packed2),
+                                       (far, [], False, packed2), (near, mate, True, packed3),
+                                       (near, mate, False, packed3)):
+        wait("G", *packed)
+        n = len(out_engines) // len(ranks)
+        tr = [transfer(d, out_engines[n * i:n * i + n], codes) for i, d in enumerate(ranks)]
+        tr += [transfer(d, home_engines, codes) for d in home]
+        g.remote_dma_fused(tr, local_sem=sem.loc)
+        local += n * len(ranks) + len(home_engines) * len(home)
+        if home:
+            comes_b += n * len(ranks)
+            comes_a += len(home_engines) * len(home)
+        else:
+            comes_a += n * len(ranks)
 
-    xq = inc("cv", V.quantize_mx(T.xq[:, :], T.xp[:, :], T.xt[:, :]))
-    wq = []
-    for i in range(2):
-        wv("sw%d" % i, 16)
-        wq.append(inc("cv", V.quantize_mx(T.wq[:, 512 * i:512 * i + 512], T.wp[:, 512 * i:512 * i + 512],
-                                          T.wt[:, 2048 * i:2048 * i + 2048])))
-    wv("sm", 128)
-    offm = inc("cv", V.tensor_scalar(T.offm[:, :], T.lm[:, :], 1.0, None, AluOpType.add))
+    def product(k, bank, q, p, a, b):
+        return inc("ct", P.matmul_mx(T.ps[:, 512 * bank:512 * bank + b - a], T.wq[:, 128 * k:128 * k + 128],
+                                     T.wp[:, 128 * k:128 * k + 128], q[:, a:b], p[:, a:b], True, True))
 
-    def product(k, q, p, n):
-        return inc("ct", P.matmul_mx(T.ps[:, 512 * k:512 * k + n], T.wq[:, 128 * k:128 * k + 128],
-                                     T.wp[:, 128 * k:128 * k + 128], q[:, 0:n], p[:, 0:n], True, True))
+    full = {k: [offm, zeros] for k in range(MAPS)}
 
-    def copy(k, a, to, n, vector):
-        dst, src = T.win[:, k * STRIDE + to:k * STRIDE + to + n], T.ps[:, 512 * k + a:512 * k + a + n]
-        if vector:
-            return "cv", inc("cv", V.tensor_copy(dst, src))
-        return "cs", inc("cs", S.activation(dst, src, Copy))
+    def copy(name, m, k, bank, a, to, n):
+        wait(name, *m)
+        dst, src = T.win[:, k * STRIDE + to:k * STRIDE + to + n], T.ps[:, 512 * bank + a:512 * bank + a + n]
+        done = inc("cv", V.tensor_copy(dst, src)) if name == "V" else inc("cs", S.activation(dst, src, Copy))
+        full[k].append(done)
+        return done
 
-    done = [None] * MAPS
+    def copy_slots(name, m, k, bank, ranks):
+        for i, s, n in runs(ranks):
+            done = copy(name, m, k, bank, CAP * i, 1 + COLS + CAP * s, CAP * n)
+        return done
+
+    free = {}
     for k in range(MAPS):
-        wait("P", P, "cv", wq[k // 4])
-        m = product(k, T.xq, T.xp, COLS)
-        (wv if k % 2 == 0 else ws)("ct", m)
-        done[k] = copy(k, 0, 1, COLS, k % 2 == 0)
-    wait("P", P, "arra", 2 * len(out_engines) // len(far) * len(far) + 2 * len(home_engines))
-    first = sorted(far + mate)
-    for k in range(MAPS):
-        wait("P", P, *done[k])
-        m = product(k, T.aq, T.ap, FAR)
-        (wv if k % 2 == 0 else ws)("ct", m)
-        for i, s, n in runs(first):
-            done[k] = copy(k, CAP * i, 1 + COLS + CAP * s, CAP * n, k % 2 == 0)
-    wait("P", P, "arrb", 2 * len(out_engines) // len(near) * len(near))
-    last = []
-    for k in range(MAPS):
-        wait("P", P, *done[k])
-        last.append(product(k, T.bq, T.bp, NEAR))
-    slots = 1 + COLS + CAP * near[0]
-    full = {}
+        wait("P", *xq)
+        wait("P", *wq[k])
+        m = product(k, k, T.xq, T.xp, 0, COLS)
+        free[k] = copy("V" if k in (3, 5, 7) else "S", m, k, k, 0, 1, COLS)
+    na = CAP * len(first)
+    wait("P", "arra", comes_a)
+    for k, name in EARLY:
+        wait("P", *free[k])
+        copy_slots(name, product(k, k, T.aq, T.ap, 0, na), k, k, first)
+    wait("P", "arrb", comes_b)
+    for k, name in EARLY:
+        bank = MAPS - len(EARLY) + k
+        wait("P", *free[bank])
+        free[bank] = copy_slots(name, product(k, bank, T.aq, T.ap, na, b3), k, bank, near)
 
-    def finish(k, vector):
-        (wv if vector else ws)("ct", last[k])
-        full[k] = [done[k], copy(k, 0, slots, NEAR, vector)]
+    def pick(name, k, c):
+        for need in full[k]:
+            wait(name, *need)
+        o = 32 * k + 16 * c
+        return T.win[:, k * STRIDE:k * STRIDE + WIN].indirect(T.offm[:, o:o + 16])
 
-    def ready(name, eng, k):
-        wait(name, eng, "cv", offm)
-        wait(name, eng, "cv", zeros)
-        for s, n in full[k]:
-            wait(name, eng, s, n)
-
-    def pick(k, a=0, b=COLS):
-        return T.win[:, k * STRIDE:k * STRIDE + WIN].indirect(T.offm[:, 32 * k + a // 16:32 * k + b // 16])
-
-    finish(0, False)
-    finish(1, True)
-    half = COLS // 2
-    ready("S", S, 0)
-    a0 = inc("cs", S.activation(T.g0[:, 0:half], pick(0, 0, half), Copy))
-    ready("V", V, 0)
-    a1 = inc("cv", V.tensor_copy(T.g0[:, half:], pick(0, half, COLS)))
-    finish(3, False)
-    finish(2, False)
-    ready("S", S, 2)
-    a2 = inc("cs", S.activation(T.g2[:, :], pick(2), Copy))
-    for k in (4, 5, 6, 7):
-        finish(k, False)
-
-    def add(k, out, other):
-        ready("V", V, k)
-        return inc("cv", V.tensor_tensor(out[:, :], pick(k), other[:, :], AluOpType.add))
-
-    wv("cs", a0)
-    wv("cv", a1)
-    c0 = add(1, T.acc0, T.g0)
-    wv("cs", a2)
-    c1 = add(3, T.acc1, T.g2)
-    for k0, k1 in ((4, 5), (6, 7)):
-        wv("cv", c0)
-        c0 = add(k0, T.acc0, T.acc0)
-        wv("cv", c1)
-        c1 = add(k1, T.acc1, T.acc1)
-    wv("cv", c1)
-    for i, (name, eng) in enumerate((("Y", Y), ("S", S))):
-        c = slice(half * i, half * i + half)
-        n = inc("cv", V.tensor_tensor(T.yt[:, c], T.acc0[:, c], T.acc1[:, c], AluOpType.add))
-        wait(name, eng, "cv", n)
-        eng.dma_start(T.y[:, c], T.yt[:, c]).then_inc(sem.sy, 16)
-    wait("G", g, "loc", local)
+    halves = [slice(0, HALF), slice(HALF, COLS)]
+    acc = [inc("cs", S.activation(T.g0[:, halves[c]], pick("S", 0, c), Copy)) for c in range(2)]
+    for k in range(len(EARLY), MAPS):
+        wait("P", *free[k])
+        copy_slots("S", product(k, k, T.aq, T.ap, 0, b3), k, k, order)
+    for k in range(1, MAPS):
+        other = T.g0 if k == 1 else T.acc
+        for c in range(2):
+            wait("V", *acc[c])
+            acc[c] = inc("cv", V.tensor_tensor(T.acc[:, halves[c]], pick("V", k, c), other[:, halves[c]], AluOpType.add))
+    for c, name in ((0, "Y"), (1, "S")):
+        wait(name, *acc[c])
+        queue[name].dma_start(T.y[:, halves[c]], T.acc[:, halves[c]]).then_inc(sem.sy, 16)
+    wait("G", "loc", local)
     Y.wait_ge(sem.sy, 32)

from concourse.bass import DstId, RemoteDMATransfer
from concourse.mybir import dt, AluOpType, ActivationFunctionType

COLS, MAPS, CAP = 512, 8, 64
STRIDE = 1028
WIN = 1 + 2 * COLS
HALF = COLS // 2
EARLY = ((0, "S"), (1, "V"), (2, "V"))

SCRATCH = {
    "xt": ("sbuf", [128, 4 * COLS], "bfloat16"),
    "wt": ("sbuf", [128, 512 * MAPS], "bfloat16"),
    "ls": ("sbuf", [128, 32], "int32"),
    "lm": ("sbuf", [128, 256], "int32"),
    "offs": ("sbuf", [128, 32], "uint16"),
    "offm": ("sbuf", [128, 256], "uint16"),
    "h": ("sbuf", [128, 4 * 7 * CAP], "bfloat16"),
    "hq": ("sbuf", [128, 7 * CAP], "float8_e4m3fn_x4"),
    "hp": ("sbuf", [128, 7 * CAP], "uint8"),
    "xq": ("sbuf", [128, COLS], "float8_e4m3fn_x4"),
    "xp": ("sbuf", [128, COLS], "uint8"),
    "wq": ("sbuf", [128, 128 * MAPS], "float8_e4m3fn_x4"),
    "wp": ("sbuf", [128, 128 * MAPS], "uint8"),
    "aq": ("sbuf", [128, 7 * CAP], "float8_e4m3fn_x4"),
    "ap": ("sbuf", [128, 7 * CAP], "uint8"),
    "win": ("sbuf", [128, STRIDE * MAPS], "float32"),
    "g0": ("sbuf", [128, COLS], "float32"),
    "acc": ("sbuf", [128, COLS], "float32"),
    "ps": ("psum", [128, 512 * MAPS], "float32"),
}
SEMAPHORES = ["sl", "sx", "sw0", "sw1", "sw2", "sm", "sy", "cv", "cs", "ct", "arra", "arrb", "loc"]


def groups(T, topo, r):
    me = topo.chip(T.cores[r])
    far, near, mate = [], [], []
    for i in range(1, len(T.cores)):
        s = (r + i) % len(T.cores)
        c = topo.chip(T.cores[s])
        if c == me:
            mate.append(s)
        elif topo.same_plane(me, c):
            near.append(s)
        else:
            far.append(s)
    return far, sorted(near), mate


def runs(ranks):
    out = []
    for i, s in enumerate(ranks):
        if out and out[-1][1] + out[-1][2] == s:
            out[-1] = (out[-1][0], out[-1][1], out[-1][2] + 1)
        else:
            out.append((i, s, 1))
    return out


def mask_of(engines):
    m = 0
    for e in engines:
        m |= 1 << e
    return m


def rank_program(g, core, T, topo):
    r = T.rank_of(core)
    if r is None:
        return
    sem = T.sem
    V, S, P, Y = g.vector, g.scalar, g.tensor, g.sync
    queue = {"V": V, "S": S, "P": P, "Y": Y, "G": g}
    Copy = ActivationFunctionType.Copy
    cnt = {"cv": 0, "cs": 0, "ct": 0}
    seen = {}

    def wait(name, s, n):
        if seen.get((name, s), 0) < n:
            queue[name].wait_ge(sem[s], n)
            seen[(name, s)] = n

    def inc(s, call):
        call.then_inc(sem[s], 1)
        cnt[s] += 1
        return s, cnt[s]

    far, near, mate = groups(T, topo, r)
    dests = far + near + mate
    cut = len(far) // 2
    first = sorted(far + mate)
    order = first + near

    for i in range(4):
        Y.dma_start(T.ls[16 * i:16 * i + 16, :], T.send[:, :]).then_inc(sem.sl, 16)
        S.dma_start(T.ls[64 + 16 * i:80 + 16 * i, :], T.send[:, :]).then_inc(sem.sl, 16)
    Y.dma_start(T.xt[:, 0:1024], T.x[:, 0:1024]).then_inc(sem.sx, 16)
    S.dma_start(T.xt[:, 1024:2048], T.x[:, 1024:2048]).then_inc(sem.sx, 16)
    wparts = ((0, 2), (2, 4), (4, 8))
    for i, (a, b) in enumerate(wparts):
        Y.dma_start(T.wt[:, 512 * a:512 * b], T.w[:, 512 * a:512 * b]).then_inc(sem["sw%d" % i], 16)
    for i in range(8):
        Y.dma_start(T.lm[16 * i:16 * i + 16, :], T.mp[:, :]).then_inc(sem.sm, 16)

    for k in range(MAPS):
        inc("cv", V.memset(T.win[:, k * STRIDE:k * STRIDE + 1], 0.0))
        o = k * STRIDE + 1 + COLS + CAP * r
        zeros = inc("cv", V.memset(T.win[:, o:o + CAP], 0.0))

    wait("V", "sl", 128)
    for i, d, n in runs(dests):
        offs = inc("cv", V.tensor_scalar(T.offs[:, 4 * i:4 * (i + n)], T.ls[:, 4 * d:4 * (d + n)], 4.0, 0.0,
                                         AluOpType.mult, AluOpType.max))

    def gather(name, lo, hi, t):
        wait(name, *offs)
        wait(name, "sx", 32)
        out = T.h[:, 4 * lo + t:4 * hi:4]
        src = T.xt[:, t:4 * COLS].indirect(T.offs[:, lo // 16:hi // 16])
        if name == "V":
            return inc("cv", V.tensor_copy(out, src))
        return inc("cs", S.activation(out, src, Copy))

    def pack(lo, hi, parts):
        for p in parts:
            wait("V", *p)
        return inc("cv", V.quantize_mx(T.hq[:, lo:hi], T.hp[:, lo:hi], T.h[:, 4 * lo:4 * hi]))

    def pack_w(i):
        a, b = wparts[i]
        wait("V", "sw%d" % i, 16)
        n = inc("cv", V.quantize_mx(T.wq[:, 128 * a:128 * b], T.wp[:, 128 * a:128 * b], T.wt[:, 512 * a:512 * b]))
        return {k: n for k in range(a, b)}

    b1, b2, b3 = CAP * cut, CAP * len(far), CAP * len(dests)
    parts = [gather("V", 0, b1, 0), gather("V", 0, b1, 1), gather("S", 0, b1, 2), gather("S", 0, b1, 3)]
    packed1 = pack(0, b1, parts)
    parts = [gather("V", b1, b2, 0), gather("V", b1, b2, 1), gather("S", b1, b2, 2), gather("S", b1, b2, 3)]
    packed2 = pack(b1, b2, parts)
    parts = [gather("V", b2, b3, 0)] + [gather("S", b2, b3, t) for t in (1, 2, 3)]
    xq = inc("cv", V.quantize_mx(T.xq[:, :], T.xp[:, :], T.xt[:, :]))
    packed3 = pack(b2, b3, parts)
    wq = pack_w(0)
    wq.update(pack_w(1))
    wq.update(pack_w(2))
    wait("V", "sm", 128)
    offm = inc("cv", V.tensor_scalar(T.offm[:, :], T.lm[:, :], 1.0, None, AluOpType.add))

    out_engines = topo.engines(core, T.cores[far[0]])
    home_engines = [e for e in topo.engines(core, T.cores[mate[0]]) if e not in out_engines][:2]

    def transfer(d, engines, codes):
        dfar, dnear, dmate = groups(T, topo, d)
        rid, pid, _ = topo.addr(T.cores[d])
        a = CAP * dests.index(d)
        p = CAP * (sorted(dfar + dmate) + dnear).index(r)
        if codes:
            src, dst = T.hq[:, a:a + CAP].bitcast(dt.uint8), T.aq[:, p:p + CAP].bitcast(dt.uint8)
        else:
            src, dst = T.hp[:, a:a + CAP], T.ap[:, p:p + CAP]
        return RemoteDMATransfer(dst_ids=[DstId(rid=rid, pnc=pid)], dma_engine_mask=mask_of(engines),
                                 remote_sem=sem.arrb if r in dnear else sem.arra, src=src, dst=dst)

    local, comes_a, comes_b = 0, 0, 0
    for ranks, home, codes, packed in ((far[:cut], [], True, packed1), (far[cut:], [], True, packed2),
                                       (far, [], False, packed2), (near, mate, True, packed3),
                                       (near, mate, False, packed3)):
        wait("G", *packed)
        n = len(out_engines) // len(ranks)
        tr = [transfer(d, out_engines[n * i:n * i + n], codes) for i, d in enumerate(ranks)]
        tr += [transfer(d, home_engines, codes) for d in home]
        g.remote_dma_fused(tr, local_sem=sem.loc)
        local += n * len(ranks) + len(home_engines) * len(home)
        if home:
            comes_b += n * len(ranks)
            comes_a += len(home_engines) * len(home)
        else:
            comes_a += n * len(ranks)

    def product(k, bank, q, p, a, b):
        return inc("ct", P.matmul_mx(T.ps[:, 512 * bank:512 * bank + b - a], T.wq[:, 128 * k:128 * k + 128],
                                     T.wp[:, 128 * k:128 * k + 128], q[:, a:b], p[:, a:b], True, True))

    full = {k: [offm, zeros] for k in range(MAPS)}

    def copy(name, m, k, bank, a, to, n):
        wait(name, *m)
        dst, src = T.win[:, k * STRIDE + to:k * STRIDE + to + n], T.ps[:, 512 * bank + a:512 * bank + a + n]
        done = inc("cv", V.tensor_copy(dst, src)) if name == "V" else inc("cs", S.activation(dst, src, Copy))
        full[k].append(done)
        return done

    def copy_slots(name, m, k, bank, ranks):
        for i, s, n in runs(ranks):
            done = copy(name, m, k, bank, CAP * i, 1 + COLS + CAP * s, CAP * n)
        return done

    free = {}
    for k in range(MAPS):
        wait("P", *xq)
        wait("P", *wq[k])
        m = product(k, k, T.xq, T.xp, 0, COLS)
        free[k] = copy("V" if k in (3, 5, 7) else "S", m, k, k, 0, 1, COLS)
    na = CAP * len(first)
    wait("P", "arra", comes_a)
    for k, name in EARLY:
        wait("P", *free[k])
        copy_slots(name, product(k, k, T.aq, T.ap, 0, na), k, k, first)
    wait("P", "arrb", comes_b)
    for k, name in EARLY:
        bank = MAPS - len(EARLY) + k
        wait("P", *free[bank])
        free[bank] = copy_slots(name, product(k, bank, T.aq, T.ap, na, b3), k, bank, near)

    def pick(name, k, c):
        for need in full[k]:
            wait(name, *need)
        o = 32 * k + 16 * c
        return T.win[:, k * STRIDE:k * STRIDE + WIN].indirect(T.offm[:, o:o + 16])

    halves = [slice(0, HALF), slice(HALF, COLS)]
    acc = [inc("cs", S.activation(T.g0[:, halves[c]], pick("S", 0, c), Copy)) for c in range(2)]
    for k in range(len(EARLY), MAPS):
        wait("P", *free[k])
        copy_slots("S", product(k, k, T.aq, T.ap, 0, b3), k, k, order)
    for k in range(1, MAPS):
        other = T.g0 if k == 1 else T.acc
        for c in range(2):
            wait("V", *acc[c])
            acc[c] = inc("cv", V.tensor_tensor(T.acc[:, halves[c]], pick("V", k, c), other[:, halves[c]], AluOpType.add))
    for c, name in ((0, "Y"), (1, "S")):
        wait(name, *acc[c])
        queue[name].dma_start(T.y[:, halves[c]], T.acc[:, halves[c]]).then_inc(sem.sy, 16)
    wait("G", "loc", local)
    Y.wait_ge(sem.sy, 32)
